import numpy as np
import ml_dtypes


def mxq(x, axis, fmt="e4m3"):
    dtype, down = {"e4m3": (ml_dtypes.float8_e4m3fn, 7), "e5m2": (ml_dtypes.float8_e5m2, 14)}[fmt]
    v = np.moveaxis(np.asarray(x, np.float32).astype(ml_dtypes.bfloat16).astype(np.float64), axis, -1)
    blocks = v.reshape(v.shape[:-1] + (-1, 32))
    amax = np.abs(blocks).max(-1, keepdims=True)
    byte = np.maximum(np.where(amax > 0, np.frexp(amax)[1] - 1 + 127, 0) - down, 1)
    scale = np.exp2(byte - 127.0)
    codes = (blocks / scale).astype(np.float32).astype(dtype).astype(np.float64)
    return np.moveaxis((codes * scale).reshape(v.shape), -1, axis)


WIDE = False


def mx_kscale(k):
    if not WIDE:
        return np.ones(k)
    levels = np.array([10, -10, 5, -5, 0])
    if k % 512:
        return np.exp2(np.random.permutation(np.resize(levels, k // 32))).repeat(32)
    a = np.empty((k // 512, 16))
    for p in range(k // 512):
        a[p, :8] = np.random.permutation(np.resize(levels, 8))
        for g in range(8):
            far = levels[np.abs(levels - a[p, g]) >= 10]
            a[p, g + 8] = far[np.random.randint(len(far))]
    return np.exp2(a.ravel()).repeat(32)


def f64(x):
    return np.asarray(x).astype(np.float64)


def striped(idx):
    return np.tile(idx.reshape(-1, 16).T, (8, 1)).astype(np.uint16)


def unstriped(offs):
    return offs[:16].T.reshape(-1).astype(np.int64)


def pack_weight(w):
    k, n = w.shape
    w = f64(np.asarray(w, np.float32).astype(ml_dtypes.bfloat16)).reshape(k // 32, 32, n)
    amax = np.abs(w).max(1)
    byte = np.clip(np.where(amax > 0, np.frexp(amax)[1] - 1 + 127 - 7, 1), 1, 254)
    scaled = (w * np.exp2(127.0 - byte)[:, None, :]).reshape(k, n).astype(np.float32)
    words = np.ascontiguousarray(scaled.reshape(k // 512, 128, 4, n).transpose(0, 1, 3, 2)).astype(ml_dtypes.float8_e4m3fn).view(np.uint8)
    return words, np.ascontiguousarray(byte.astype(np.uint8).reshape(k // 512, 16, n))


def unpack_weight(words, scales):
    g, p, n, _ = words.shape
    vals = np.ascontiguousarray(words).view(ml_dtypes.float8_e4m3fn).astype(np.float64) * np.repeat(np.exp2(scales.astype(np.float64) - 127.0), 8, axis=1)[..., None]
    return vals.transpose(0, 1, 3, 2).reshape(g * 512, n)


def relu(v):
    return np.maximum(v, 0.0)


K, T, S, H, N, U, V = 1024, 2048, 1024, 512, 256, 1024, 512


def setup_inputs():
    n = np.random.standard_normal
    s = mx_kscale(K)[:, None]
    u = mx_kscale(H)
    packed_w3 = pack_weight(n((H, N)) / np.sqrt(H) / u[:, None])
    return {
        "xT": (n((K, T)) * s).astype(np.float32),
        "w1": (n((K, H)) / np.sqrt(K) / s * u).astype(np.float32),
        "w2": (n((K, H)) / np.sqrt(K) / s * u).astype(np.float32),
        "w3_words": packed_w3[0],
        "w3_scales": packed_w3[1],
        "offs": striped(np.random.permutation(T)[:S]),
        "near": striped(np.random.permutation(U)[:V]),
        "far": striped(np.random.permutation(U)[:V]),
    }


def reference(xT, w1, w2, w3_words, w3_scales, offs, near, far):
    xq = mxq(f64(xT)[:, unstriped(offs)], 0, "e4m3")
    a = np.zeros((H, S))
    a[:, unstriped(near)] = relu(mxq(f64(w1), 0, "e4m3").T @ xq[:, :V])
    e = np.zeros((H, S))
    e[:, unstriped(far)] = relu(mxq(f64(w2), 0, "e4m3").T @ xq[:, V:2 * V])
    z = np.maximum(a, e)
    return unpack_weight(w3_words, w3_scales).T @ mxq(z, 0, "e4m3")

@@ -1,0 +1,237 @@
+from contextlib import ExitStack
+
+import concourse.mybir as mybir
+
+K, T, S, H, N, V = 1024, 2048, 1024, 512, 256, 512
+FLOPS = 2 * (2 * K * H * V) + 2 * H * N * S
+
+F32 = mybir.dt.float32
+BF16 = mybir.dt.bfloat16
+I32 = mybir.dt.int32
+U32 = mybir.dt.uint32
+U16 = mybir.dt.uint16
+U8 = mybir.dt.uint8
+FP8X4 = mybir.dt.float8_e4m3fn_x4
+RELU = mybir.ActivationFunctionType.Relu
+MAX = mybir.AluOpType.max
+
+P = 128
+PACK = 4
+K_PASS = P * PACK
+PASSES = K // K_PASS
+SENSORS = 2
+X_COLS = T // 2
+CHUNK = 256
+CHUNKS = S // CHUNK
+X_VECTOR_COLS = 128
+X_VECTOR_COLS_LAST = 640
+
+
+def tile_picked_bev_max_e_kernel(
+    tc, xT, w1, w2, w3_words, w3_scales, offs, near, far, out
+):
+    nc = tc.nc
+    with ExitStack() as ctx:
+        held = ctx.enter_context(tc.tile_pool(name="held", bufs=1))
+        raw = ctx.enter_context(tc.tile_pool(name="raw", bufs=6))
+        ring = ctx.enter_context(tc.tile_pool(name="ring", bufs=2))
+        psum = ctx.enter_context(tc.psum_pool(name="psum", bufs=1))
+
+        offs_sb = held.tile([P, S // 16], U16, name="offs_sb")
+        cell_lists = [held.tile([P, V // 16], U16, name="cells%d" % s) for s in range(SENSORS)]
+
+        warm_in = held.tile([P, 2], F32, name="warm_in")
+        warm_out = held.tile([P, 2], F32, name="warm_out")
+        nc.vector.memset(warm_in[:], 0.0)
+        nc.scalar.activation(warm_out[:], warm_in[:], RELU)
+
+        maps = [[held.tile([P, S], F32, name="map%d_%d" % (s, t)) for t in range(PACK)] for s in range(SENSORS)]
+        for s in range(SENSORS):
+            for t in range(PACK):
+                nc.vector.memset(maps[s][t][:].bitcast(I32), 0)
+        w3_codes = held.tile([P, N], U32, name="w3_codes", align_bytes=64)
+        w3_scale = held.tile([P, N], U8, name="w3_scale", align_bytes=64)
+        nc.vector.memset(w3_scale[:].bitcast(I32), 0)
+
+        pairs = [[held.tile([P, 2 * T], BF16, name="pairs%d_%d" % (g, u)) for u in range(2)] for g in range(PASSES)]
+        x_codes = [[held.tile([P, V], U32, name="xc%d_%d" % (g, s), align_bytes=64) for s in range(SENSORS)] for g in range(PASSES)]
+        x_scale = [[held.tile([P, V], U8, name="xs%d_%d" % (g, s), align_bytes=64) for s in range(SENSORS)] for g in range(PASSES)]
+        picked = [[held.tile([P, 2, V], U32, name="pk%d_%d" % (g, s)) for s in range(SENSORS)] for g in range(PASSES)]
+        w_codes = [[held.tile([P, H], U32, name="wc%d_%d" % (s, g), align_bytes=64) for g in range(PASSES)] for s in range(SENSORS)]
+        w_scale = [[held.tile([P, H], U8, name="ws%d_%d" % (s, g), align_bytes=64) for g in range(PASSES)] for s in range(SENSORS)]
+
+        def copy_on(engine, dst, src):
+            if engine == "vector":
+                nc.vector.tensor_copy(dst, src)
+            else:
+                nc.scalar.copy(dst, src)
+
+        def load_x(g, u, h):
+            piece = raw.tile([P, 2, X_COLS], F32, name="piece", tag="raw")
+            rows = xT[g * K_PASS : (g + 1) * K_PASS, :].rearrange("(p j) c -> p j c", j=PACK)
+            nc.sync.dma_start(out=piece[:], in_=rows[:, 2 * u : 2 * u + 2, h * X_COLS : (h + 1) * X_COLS])
+            return piece
+
+        def round_x(piece, g, u, h, vector_cols):
+            dst = pairs[g][u][:].rearrange("p (c e) -> p c e", e=2)
+            for engine, c0, c1 in (("scalar", vector_cols, X_COLS), ("vector", 0, vector_cols)):
+                copy_on(engine, dst[:, h * X_COLS + c0 : h * X_COLS + c1, :], piece[:, :, c0:c1].rearrange("p e c -> p c e"))
+
+        def gather_x(g, u, s):
+            nc.vector.tensor_copy(
+                picked[g][s][:, u, :],
+                pairs[g][u][:].bitcast(U32).indirect(offs_sb[:, s * (V // 16) : (s + 1) * (V // 16)]),
+            )
+
+        def weave_x(g, s, engine, woven=None):
+            if woven is None:
+                woven = ring.tile([P, PACK * V], BF16, name="woven", align_bytes=64)
+            if engine == "vector":
+                nc.vector.tensor_copy(
+                    woven[:].bitcast(I32).rearrange("p (n u) -> p n u", u=2),
+                    picked[g][s][:].bitcast(I32).rearrange("p u n -> p n u"),
+                )
+            else:
+                nc.scalar.copy(
+                    woven[:].rearrange("p (n u e) -> p n u e", u=2, e=2),
+                    picked[g][s][:].bitcast(BF16).rearrange("p u (n e) -> p n u e", e=2),
+                )
+            return woven
+
+        def quantize_x(woven, g, s):
+            nc.vector.quantize_mx(out=x_codes[g][s][:].bitcast(FP8X4), scales=x_scale[g][s][:], in_=woven[:])
+
+        def load_w(w, g, c0, c1, piece=None):
+            if piece is None:
+                piece = raw.tile([P, PACK, c1 - c0], F32, name="wpiece", tag="raw")
+            rows = w[g * K_PASS : (g + 1) * K_PASS, :].rearrange("(p j) c -> p j c", j=PACK)
+            nc.sync.dma_start(out=piece[:], in_=rows[:, :, c0:c1])
+            return piece
+
+        def round_w(engine, dealt, piece, piece_c0, c0, c1):
+            dst = dealt[:].rearrange("p (t m j) -> p m j t", t=PACK, j=PACK)
+            src = piece[:, :, c0 - piece_c0 : c1 - piece_c0].rearrange("p j (m t) -> p m j t", t=PACK)
+            copy_on(engine, dst[:, c0 // PACK : c1 // PACK, :, :], src)
+
+        def quantize_w(dealt, s, g):
+            nc.vector.quantize_mx(out=w_codes[s][g][:].bitcast(FP8X4), scales=w_scale[s][g][:], in_=dealt[:])
+
+        def first_layer_pass(acc, s, t, g):
+            cols = slice(t * P, (t + 1) * P)
+            nc.tensor.matmul_mx(
+                out=acc[:],
+                lhsT=w_codes[s][g][:, cols].bitcast(FP8X4),
+                lhsT_scale=w_scale[s][g][:, cols],
+                rhs=x_codes[g][s][:].bitcast(FP8X4),
+                rhs_scale=x_scale[g][s][:],
+                start=(g == 0),
+                stop=(g == PASSES - 1),
+            )
+
+        x_steps = [(g, u, h) for g in range(PASSES) for u in range(2) for h in range(2)]
+        for i, (g, u, h) in enumerate(x_steps):
+            piece = load_x(g, u, h)
+            if i == 0:
+                nc.sync.dma_start(offs_sb[:], offs)
+            last = i == len(x_steps) - 1
+            round_x(piece, g, u, h, X_VECTOR_COLS_LAST if last else X_VECTOR_COLS)
+            if h == 1 and not last:
+                for s in range(SENSORS):
+                    gather_x(g, u, s)
+                if u == 1:
+                    woven = [weave_x(g, s, "vector") for s in range(SENSORS)]
+                    for s in range(SENSORS):
+                        quantize_x(woven[s], g, s)
+        g_last = PASSES - 1
+        gather_x(g_last, 1, 0)
+        quantize_x(weave_x(g_last, 0, "vector"), g_last, 0)
+
+        dealt = [[held.tile([P, PACK * H], BF16, name="dealt%d_%d" % (s, g), tag="dealt%d_%d" % (s, g), align_bytes=64) for g in range(PASSES)] for s in range(SENSORS)]
+        piece = load_w(w1, 0, 0, H)
+        nc.sync.dma_start(cell_lists[0][:], near)
+        round_w("scalar", dealt[0][0], piece, 0, 0, H)
+        quantize_w(dealt[0][0], 0, 0)
+        piece = load_w(w1, 1, 0, H // 2)
+        round_w("scalar", dealt[0][1], piece, 0, 0, H // 2)
+        piece = load_w(w1, 1, H // 2, H)
+        round_w("scalar", dealt[0][1], piece, H // 2, H // 2, H // 2 + 64)
+        round_w("vector", dealt[0][1], piece, H // 2, H // 2 + 64, H)
+        quantize_w(dealt[0][1], 0, 1)
+        gather_x(g_last, 1, 1)
+        woven_last = held.tile([P, PACK * V], BF16, name="woven_last", tag="dealt0_1", align_bytes=64)
+        quantize_x(weave_x(g_last, 1, "vector", woven_last), g_last, 1)
+
+        banks = [[psum.tile([P, V], F32, name="acc%d_%d" % (s, t), tag="bank%d" % (s * PACK + t)) for t in range(PACK)] for s in range(SENSORS)]
+
+        def scatter(s, t, values):
+            nc.vector.tensor_copy(maps[s][t][:].indirect(cell_lists[s][:]), values[:])
+
+        for g in range(PASSES):
+            for t in range(PACK):
+                first_layer_pass(banks[0][t], 0, t, g)
+        early = [held.tile([P, V], F32, name="res0_%d" % t) for t in range(2)]
+        for t in range(2):
+            nc.scalar.activation(early[t][:], banks[0][t][:], RELU)
+
+        w2_pieces = [
+            load_w(w2, g, 0, H, held.tile([P, PACK, H], F32, name="w2raw%d" % g, tag="w2raw%d" % g)) for g in range(PASSES)
+        ]
+        nc.sync.dma_start(cell_lists[1][:], far)
+        nc.sync.dma_start(out=w3_codes[:].bitcast(I32), in_=w3_words[0].rearrange("p n r -> p (n r)").bitcast(I32))
+        for q in range(4):
+            nc.sync.dma_start(
+                out=w3_scale[32 * q : 32 * q + 4, :].bitcast(I32), in_=w3_scales[0, 4 * q : 4 * q + 4, :].bitcast(I32)
+            )
+        for g in range(PASSES):
+            round_w("scalar", dealt[1][g], w2_pieces[g], 0, 0, H)
+
+        scatter(0, 0, early[0])
+        scatter(0, 1, early[1])
+        for g in range(PASSES):
+            quantize_w(dealt[1][g], 1, g)
+        late = held.tile([P, 2, V], F32, name="late", tag="w2raw1")
+        for t in range(2, PACK):
+            nc.scalar.activation(late[:, t - 2, :], banks[0][t][:], RELU)
+            nc.vector.tensor_copy(maps[0][t][:].indirect(cell_lists[0][:]), late[:, t - 2, :])
+        for g in range(PASSES):
+            for t in range(PACK):
+                first_layer_pass(banks[1][t], 1, t, g)
+
+        z_planes = [held.tile([P, PACK, CHUNK], BF16, name="zp%d" % c) for c in range(CHUNKS)]
+        for t in range(PACK):
+            values = ring.tile([P, V], F32, name="values")
+            nc.scalar.activation(values[:], banks[1][t][:], RELU)
+            scatter(1, t, values)
+            for c in range(CHUNKS):
+                cells = slice(c * CHUNK, (c + 1) * CHUNK)
+                nc.vector.tensor_tensor(z_planes[c][:, t, :], maps[0][t][:, cells], maps[1][t][:, cells], MAX)
+
+        out_rows = out.rearrange("(m p) r -> p m r", p=P)
+        z_woven = []
+        for c in range(CHUNKS):
+            zw = held.tile([P, PACK * CHUNK], BF16, name="zw%d" % c, align_bytes=64)
+            copy_on(
+                "scalar" if c % 2 == 0 else "vector",
+                zw[:].rearrange("p (c i t) -> p c t i", i=4, t=PACK),
+                z_planes[c][:].rearrange("p t (c i) -> p c t i", i=4),
+            )
+            z_woven.append(zw)
+        for c in (1, 0, 3, 2):
+            z_codes = held.tile([P, CHUNK], U32, name="zc%d" % c, align_bytes=64)
+            z_scale = held.tile([P, CHUNK], U8, name="zs%d" % c, align_bytes=64)
+            nc.vector.quantize_mx(out=z_codes[:].bitcast(FP8X4), scales=z_scale[:], in_=z_woven[c][:])
+            acc = psum.tile([P, N // P, CHUNK], F32, name="oacc%d" % c, tag="bank%d" % c)
+            for m in range(N // P):
+                cols = slice(m * P, (m + 1) * P)
+                nc.tensor.matmul_mx(
+                    out=acc[:, m, :],
+                    lhsT=w3_codes[:, cols].bitcast(FP8X4),
+                    lhsT_scale=w3_scale[:, cols],
+                    rhs=z_codes[:].bitcast(FP8X4),
+                    rhs_scale=z_scale[:],
+                    start=True,
+                    stop=True,
+                )
+            staged = held.tile([P, N // P, CHUNK], F32, name="staged%d" % c)
+            copy_on("scalar" if c != 2 else "vector", staged[:], acc[:])
+            nc.sync.dma_start(out=out_rows[:, :, c * CHUNK : (c + 1) * CHUNK], in_=staged[:])

@@ -14,6 +14,8 @@ U8 = mybir.dt.uint8
 FP8X4 = mybir.dt.float8_e4m3fn_x4
 RELU = mybir.ActivationFunctionType.Relu
 MAX = mybir.AluOpType.max
+ADD = mybir.AluOpType.add
+SUBTRACT = mybir.AluOpType.subtract
 
 P = 128
 PACK = 4
@@ -23,8 +25,9 @@ SENSORS = 2
 X_COLS = T // 2
 CHUNK = 256
 CHUNKS = S // CHUNK
-X_VECTOR_COLS = 128
-X_VECTOR_COLS_LAST = 640
+X_VECTOR_COLS = (0, 640, 0, 640, 0, 640, 0, 640)
+W_SCALAR_COLS = 64
+GP = (4, 4, 0, 0)
 
 
 def tile_picked_bev_max_e_kernel(
@@ -33,8 +36,6 @@ def tile_picked_bev_max_e_kernel(
     nc = tc.nc
     with ExitStack() as ctx:
         held = ctx.enter_context(tc.tile_pool(name="held", bufs=1))
-        raw = ctx.enter_context(tc.tile_pool(name="raw", bufs=6))
-        ring = ctx.enter_context(tc.tile_pool(name="ring", bufs=2))
         psum = ctx.enter_context(tc.psum_pool(name="psum", bufs=1))
 
         offs_sb = held.tile([P, S // 16], U16, name="offs_sb")
@@ -46,19 +47,21 @@ def tile_picked_bev_max_e_kernel(
         nc.scalar.activation(warm_out[:], warm_in[:], RELU)
 
         maps = [[held.tile([P, S], F32, name="map%d_%d" % (s, t)) for t in range(PACK)] for s in range(SENSORS)]
-        for s in range(SENSORS):
-            for t in range(PACK):
-                nc.vector.memset(maps[s][t][:].bitcast(I32), 0)
+        for t in range(PACK):
+            nc.vector.memset(maps[0][t][:].bitcast(I32), 0)
+            nc.gpsimd.memset(maps[1][t][:].bitcast(I32), 0)
         w3_codes = held.tile([P, N], U32, name="w3_codes", align_bytes=64)
         w3_scale = held.tile([P, N], U8, name="w3_scale", align_bytes=64)
         nc.vector.memset(w3_scale[:].bitcast(I32), 0)
 
-        pairs = [[held.tile([P, 2 * T], BF16, name="pairs%d_%d" % (g, u)) for u in range(2)] for g in range(PASSES)]
-        x_codes = [[held.tile([P, V], U32, name="xc%d_%d" % (g, s), align_bytes=64) for s in range(SENSORS)] for g in range(PASSES)]
-        x_scale = [[held.tile([P, V], U8, name="xs%d_%d" % (g, s), align_bytes=64) for s in range(SENSORS)] for g in range(PASSES)]
-        picked = [[held.tile([P, 2, V], U32, name="pk%d_%d" % (g, s)) for s in range(SENSORS)] for g in range(PASSES)]
+        pairs = [[held.tile([P, 2 * T], BF16, name="pairs%d_%d" % (g, u), tag="pairs%d_%d" % (g, u)) for u in range(2)] for g in range(PASSES)]
+        x_codes = [held.tile([P, S], U32, name="xc%d" % g, align_bytes=64) for g in range(PASSES)]
+        x_scale = [held.tile([P, S], U8, name="xs%d" % g, align_bytes=64) for g in range(PASSES)]
+        picked = [held.tile([P, 2 * S], U32, name="pk%d" % g) for g in range(PASSES)]
         w_codes = [[held.tile([P, H], U32, name="wc%d_%d" % (s, g), align_bytes=64) for g in range(PASSES)] for s in range(SENSORS)]
         w_scale = [[held.tile([P, H], U8, name="ws%d_%d" % (s, g), align_bytes=64) for g in range(PASSES)] for s in range(SENSORS)]
+        dealt = [[held.tile([P, PACK * H], BF16, name="dealt%d_%d" % (s, g), align_bytes=64) for g in range(PASSES)] for s in range(SENSORS)]
+        woven = held.tile([P, PACK * S], BF16, name="woven", align_bytes=64)
 
         def copy_on(engine, dst, src):
             if engine == "vector":
@@ -67,7 +70,7 @@ def tile_picked_bev_max_e_kernel(
                 nc.scalar.copy(dst, src)
 
         def load_x(g, u, h):
-            piece = raw.tile([P, 2, X_COLS], F32, name="piece", tag="raw")
+            piece = held.tile([P, 2, X_COLS], F32, name="piece", tag="x%d" % (4 * g + 2 * u + h))
             rows = xT[g * K_PASS : (g + 1) * K_PASS, :].rearrange("(p j) c -> p j c", j=PACK)
             nc.sync.dma_start(out=piece[:], in_=rows[:, 2 * u : 2 * u + 2, h * X_COLS : (h + 1) * X_COLS])
             return piece
@@ -75,55 +78,47 @@ def tile_picked_bev_max_e_kernel(
         def round_x(piece, g, u, h, vector_cols):
             dst = pairs[g][u][:].rearrange("p (c e) -> p c e", e=2)
             for engine, c0, c1 in (("scalar", vector_cols, X_COLS), ("vector", 0, vector_cols)):
-                copy_on(engine, dst[:, h * X_COLS + c0 : h * X_COLS + c1, :], piece[:, :, c0:c1].rearrange("p e c -> p c e"))
+                if c1 > c0:
+                    copy_on(engine, dst[:, h * X_COLS + c0 : h * X_COLS + c1, :], piece[:, :, c0:c1].rearrange("p e c -> p c e"))
 
-        def gather_x(g, u, s):
+        def gather_x(g, u, n0, n1):
             nc.vector.tensor_copy(
-                picked[g][s][:, u, :],
-                pairs[g][u][:].bitcast(U32).indirect(offs_sb[:, s * (V // 16) : (s + 1) * (V // 16)]),
+                picked[g][:, u * S + n0 : u * S + n1], pairs[g][u][:].bitcast(U32).indirect(offs_sb[:, n0 // 16 : n1 // 16])
             )
 
-        def weave_x(g, s, engine, woven=None):
-            if woven is None:
-                woven = ring.tile([P, PACK * V], BF16, name="woven", align_bytes=64)
-            if engine == "vector":
-                nc.vector.tensor_copy(
-                    woven[:].bitcast(I32).rearrange("p (n u) -> p n u", u=2),
-                    picked[g][s][:].bitcast(I32).rearrange("p u n -> p n u"),
-                )
-            else:
-                nc.scalar.copy(
-                    woven[:].rearrange("p (n u e) -> p n u e", u=2, e=2),
-                    picked[g][s][:].bitcast(BF16).rearrange("p u (n e) -> p n u e", e=2),
-                )
-            return woven
+        def weave_x(g, n0, n1, dst):
+            nc.vector.tensor_copy(
+                dst.bitcast(I32).rearrange("p (n u) -> p n u", u=2),
+                picked[g][:].bitcast(I32).rearrange("p (u n) -> p n u", u=2)[:, n0:n1, :],
+            )
 
-        def quantize_x(woven, g, s):
-            nc.vector.quantize_mx(out=x_codes[g][s][:].bitcast(FP8X4), scales=x_scale[g][s][:], in_=woven[:])
+        def quantize_x(g, n0, n1, src):
+            nc.vector.quantize_mx(out=x_codes[g][:, n0:n1].bitcast(FP8X4), scales=x_scale[g][:, n0:n1], in_=src)
 
         def load_w(w, g, c0, c1, piece=None):
             if piece is None:
-                piece = raw.tile([P, PACK, c1 - c0], F32, name="wpiece", tag="raw")
+                piece = held.tile([P, PACK, c1 - c0], F32, name="w1raw%d_%d" % (g, c0))
             rows = w[g * K_PASS : (g + 1) * K_PASS, :].rearrange("(p j) c -> p j c", j=PACK)
             nc.sync.dma_start(out=piece[:], in_=rows[:, :, c0:c1])
             return piece
 
-        def round_w(engine, dealt, piece, piece_c0, c0, c1):
-            dst = dealt[:].rearrange("p (t m j) -> p m j t", t=PACK, j=PACK)
+        def round_w(engine, dst_tile, piece, piece_c0, c0, c1):
+            dst = dst_tile[:].rearrange("p (t m j) -> p m j t", t=PACK, j=PACK)
             src = piece[:, :, c0 - piece_c0 : c1 - piece_c0].rearrange("p j (m t) -> p m j t", t=PACK)
             copy_on(engine, dst[:, c0 // PACK : c1 // PACK, :, :], src)
 
-        def quantize_w(dealt, s, g):
-            nc.vector.quantize_mx(out=w_codes[s][g][:].bitcast(FP8X4), scales=w_scale[s][g][:], in_=dealt[:])
+        def quantize_w(s, g):
+            nc.vector.quantize_mx(out=w_codes[s][g][:].bitcast(FP8X4), scales=w_scale[s][g][:], in_=dealt[s][g][:])
 
         def first_layer_pass(acc, s, t, g):
             cols = slice(t * P, (t + 1) * P)
+            picks = slice(s * V, (s + 1) * V)
             nc.tensor.matmul_mx(
                 out=acc[:],
                 lhsT=w_codes[s][g][:, cols].bitcast(FP8X4),
                 lhsT_scale=w_scale[s][g][:, cols],
-                rhs=x_codes[g][s][:].bitcast(FP8X4),
-                rhs_scale=x_scale[g][s][:],
+                rhs=x_codes[g][:, picks].bitcast(FP8X4),
+                rhs_scale=x_scale[g][:, picks],
                 start=(g == 0),
                 stop=(g == PASSES - 1),
             )
@@ -133,49 +128,49 @@ def tile_picked_bev_max_e_kernel(
             piece = load_x(g, u, h)
             if i == 0:
                 nc.sync.dma_start(offs_sb[:], offs)
-            last = i == len(x_steps) - 1
-            round_x(piece, g, u, h, X_VECTOR_COLS_LAST if last else X_VECTOR_COLS)
-            if h == 1 and not last:
-                for s in range(SENSORS):
-                    gather_x(g, u, s)
+            round_x(piece, g, u, h, X_VECTOR_COLS[i])
+            if h == 1 and i < len(x_steps) - 1:
+                gather_x(g, u, 0, S)
                 if u == 1:
-                    woven = [weave_x(g, s, "vector") for s in range(SENSORS)]
-                    for s in range(SENSORS):
-                        quantize_x(woven[s], g, s)
+                    weave_x(g, 0, S, woven[:])
+                    quantize_x(g, 0, S, woven[:])
         g_last = PASSES - 1
-        gather_x(g_last, 1, 0)
-        quantize_x(weave_x(g_last, 0, "vector"), g_last, 0)
+        gather_x(g_last, 1, 0, V)
+        weave_x(g_last, 0, V, woven[:, : PACK * V])
+        quantize_x(g_last, 0, V, woven[:, : PACK * V])
+        gather_x(g_last, 1, V, S)
 
-        dealt = [[held.tile([P, PACK * H], BF16, name="dealt%d_%d" % (s, g), tag="dealt%d_%d" % (s, g), align_bytes=64) for g in range(PASSES)] for s in range(SENSORS)]
-        piece = load_w(w1, 0, 0, H)
-        nc.sync.dma_start(cell_lists[0][:], near)
-        round_w("scalar", dealt[0][0], piece, 0, 0, H)
-        quantize_w(dealt[0][0], 0, 0)
-        piece = load_w(w1, 1, 0, H // 2)
-        round_w("scalar", dealt[0][1], piece, 0, 0, H // 2)
-        piece = load_w(w1, 1, H // 2, H)
-        round_w("scalar", dealt[0][1], piece, H // 2, H // 2, H // 2 + 64)
-        round_w("vector", dealt[0][1], piece, H // 2, H // 2 + 64, H)
-        quantize_w(dealt[0][1], 0, 1)
-        gather_x(g_last, 1, 1)
-        woven_last = held.tile([P, PACK * V], BF16, name="woven_last", tag="dealt0_1", align_bytes=64)
-        quantize_x(weave_x(g_last, 1, "vector", woven_last), g_last, 1)
+        half = H // 2
+        for g in range(PASSES):
+            for c0 in (0, half):
+                piece = load_w(w1, g, c0, c0 + half)
+                if g == 0 and c0 == half:
+                    nc.sync.dma_start(cell_lists[0][:], near)
+                if g == PASSES - 1 and c0 == half:
+                    round_w("scalar", dealt[0][g], piece, c0, c0, c0 + W_SCALAR_COLS)
+                    round_w("vector", dealt[0][g], piece, c0, c0 + W_SCALAR_COLS, H)
+                else:
+                    round_w("scalar", dealt[0][g], piece, c0, c0, c0 + half)
+            quantize_w(0, g)
+        weave_x(g_last, V, S, dealt[0][g_last][:])
+        quantize_x(g_last, V, S, dealt[0][g_last][:])
 
         banks = [[psum.tile([P, V], F32, name="acc%d_%d" % (s, t), tag="bank%d" % (s * PACK + t)) for t in range(PACK)] for s in range(SENSORS)]
+        values = [held.tile([P, V], F32, name="values%d" % b) for b in range(2)]
 
-        def scatter(s, t, values):
-            nc.vector.tensor_copy(maps[s][t][:].indirect(cell_lists[s][:]), values[:])
+        def relu(s, t, dst):
+            nc.scalar.activation(dst, banks[s][t][:], RELU)
+
+        def scatter(s, t, src):
+            nc.vector.tensor_copy(maps[s][t][:].indirect(cell_lists[s][:]), src)
 
         for g in range(PASSES):
             for t in range(PACK):
                 first_layer_pass(banks[0][t], 0, t, g)
-        early = [held.tile([P, V], F32, name="res0_%d" % t) for t in range(2)]
         for t in range(2):
-            nc.scalar.activation(early[t][:], banks[0][t][:], RELU)
+            relu(0, t, values[t][:])
 
-        w2_pieces = [
-            load_w(w2, g, 0, H, held.tile([P, PACK, H], F32, name="w2raw%d" % g, tag="w2raw%d" % g)) for g in range(PASSES)
-        ]
+        w2_pieces = [load_w(w2, g, 0, H, held.tile([P, PACK, H], F32, name="w2raw%d" % g, tag="x%d" % g)) for g in range(PASSES)]
         nc.sync.dma_start(cell_lists[1][:], far)
         nc.sync.dma_start(out=w3_codes[:].bitcast(I32), in_=w3_words[0].rearrange("p n r -> p (n r)").bitcast(I32))
         for q in range(4):
@@ -185,46 +180,67 @@ def tile_picked_bev_max_e_kernel(
         for g in range(PASSES):
             round_w("scalar", dealt[1][g], w2_pieces[g], 0, 0, H)
 
-        scatter(0, 0, early[0])
-        scatter(0, 1, early[1])
+        scatter(0, 0, values[0][:])
+        scatter(0, 1, values[1][:])
         for g in range(PASSES):
-            quantize_w(dealt[1][g], 1, g)
-        late = held.tile([P, 2, V], F32, name="late", tag="w2raw1")
-        for t in range(2, PACK):
-            nc.scalar.activation(late[:, t - 2, :], banks[0][t][:], RELU)
-            nc.vector.tensor_copy(maps[0][t][:].indirect(cell_lists[0][:]), late[:, t - 2, :])
+            quantize_w(1, g)
+        late = w2_pieces[PASSES - 1][:, 0, :]
+        relu(0, 2, late)
+        scatter(0, 2, late)
         for g in range(PASSES):
             for t in range(PACK):
                 first_layer_pass(banks[1][t], 1, t, g)
 
         z_planes = [held.tile([P, PACK, CHUNK], BF16, name="zp%d" % c) for c in range(CHUNKS)]
-        for t in range(PACK):
-            values = ring.tile([P, V], F32, name="values")
-            nc.scalar.activation(values[:], banks[1][t][:], RELU)
-            scatter(1, t, values)
-            for c in range(CHUNKS):
+
+        def join(t):
+            n_gp = GP[t]
+            if n_gp:
+                cells = slice(0, n_gp * CHUNK)
+                diff = held.tile([P, 2, S], F32, name="diff%d" % t, tag="pairs%d_%d" % (t // 2, t % 2))
+                for c0 in range(0, n_gp, 2):
+                    cells = slice(c0 * CHUNK, (c0 + 2) * CHUNK)
+                    nc.gpsimd.tensor_tensor(diff[:, 0, cells], maps[0][t][:, cells], maps[1][t][:, cells], SUBTRACT)
+                    nc.scalar.activation(diff[:, 1, cells], diff[:, 0, cells], RELU)
+                for c in range(n_gp):
+                    cells = slice(c * CHUNK, (c + 1) * CHUNK)
+                    nc.gpsimd.tensor_tensor(z_planes[c][:, t, :], diff[:, 1, cells], maps[1][t][:, cells], ADD)
+            for c in range(n_gp, CHUNKS):
                 cells = slice(c * CHUNK, (c + 1) * CHUNK)
                 nc.vector.tensor_tensor(z_planes[c][:, t, :], maps[0][t][:, cells], maps[1][t][:, cells], MAX)
 
+        rest = [(1, 0), (1, 1), (0, 3), (1, 2), (1, 3)]
+        for i, (s, t) in enumerate(rest):
+            relu(s, t, values[i % 2][:])
+            scatter(s, t, values[i % 2][:])
+            if (1 - s, t) not in rest[i:]:
+                join(t)
+
         out_rows = out.rearrange("(m p) r -> p m r", p=P)
-        z_woven = []
-        for c in range(CHUNKS):
-            zw = held.tile([P, PACK * CHUNK], BF16, name="zw%d" % c, align_bytes=64)
+        z_woven = [held.tile([P, PACK * CHUNK], BF16, name="zw%d" % c, align_bytes=64) for c in range(CHUNKS)]
+
+        def weave_z(engine, c, n0, n1):
             copy_on(
-                "scalar" if c % 2 == 0 else "vector",
-                zw[:].rearrange("p (c i t) -> p c t i", i=4, t=PACK),
-                z_planes[c][:].rearrange("p t (c i) -> p c t i", i=4),
+                engine,
+                z_woven[c][:, PACK * n0 : PACK * n1].rearrange("p (c i t) -> p c t i", i=4, t=PACK),
+                z_planes[c][:, :, n0:n1].rearrange("p t (c i) -> p c t i", i=4),
             )
-            z_woven.append(zw)
-        for c in (1, 0, 3, 2):
+
+        def second_layer(c):
+            last = c == CHUNKS - 1
             z_codes = held.tile([P, CHUNK], U32, name="zc%d" % c, align_bytes=64)
             z_scale = held.tile([P, CHUNK], U8, name="zs%d" % c, align_bytes=64)
             nc.vector.quantize_mx(out=z_codes[:].bitcast(FP8X4), scales=z_scale[:], in_=z_woven[c][:])
-            acc = psum.tile([P, N // P, CHUNK], F32, name="oacc%d" % c, tag="bank%d" % c)
+            staged = held.tile([P, N // P, CHUNK], F32, name="staged%d" % c, tag="x%d" % (2 + c))
+            if last:
+                accs = [psum.tile([P, CHUNK], F32, name="oacc%d_%d" % (c, m), tag="bank%d" % (c + m))[:] for m in range(N // P)]
+            else:
+                acc = psum.tile([P, N // P, CHUNK], F32, name="oacc%d" % c, tag="bank%d" % c)
+                accs = [acc[:, m, :] for m in range(N // P)]
             for m in range(N // P):
                 cols = slice(m * P, (m + 1) * P)
                 nc.tensor.matmul_mx(
-                    out=acc[:, m, :],
+                    out=accs[m],
                     lhsT=w3_codes[:, cols].bitcast(FP8X4),
                     lhsT_scale=w3_scale[:, cols],
                     rhs=z_codes[:].bitcast(FP8X4),
@@ -232,6 +248,19 @@ def tile_picked_bev_max_e_kernel(
                     start=True,
                     stop=True,
                 )
-            staged = held.tile([P, N // P, CHUNK], F32, name="staged%d" % c)
-            copy_on("scalar" if c != 2 else "vector", staged[:], acc[:])
+            if last:
+                nc.vector.tensor_copy(staged[:, 0, :], accs[0])
+                nc.scalar.copy(staged[:, 1, :], accs[1])
+            else:
+                copy_on(("scalar", "scalar", "scalar")[c], staged[:], acc[:])
             nc.sync.dma_start(out=out_rows[:, :, c * CHUNK : (c + 1) * CHUNK], in_=staged[:])
+
+        weave_z("scalar", 0, 0, CHUNK)
+        weave_z("vector", 1, 0, CHUNK)
+        weave_z("scalar", 2, 0, CHUNK)
+        second_layer(0)
+        second_layer(1)
+        weave_z("vector", 3, 0, 160)
+        weave_z("scalar", 3, 160, CHUNK)
+        second_layer(2)
+        second_layer(3)

@@ -1,6 +1,7 @@
 from contextlib import ExitStack
 
 import concourse.mybir as mybir
+from concourse.masks import make_identity
 
 K, T, S, H, N, V = 1024, 2048, 1024, 512, 256, 512
 FLOPS = 2 * (2 * K * H * V) + 2 * H * N * S
@@ -14,8 +15,7 @@ U8 = mybir.dt.uint8
 FP8X4 = mybir.dt.float8_e4m3fn_x4
 RELU = mybir.ActivationFunctionType.Relu
 MAX = mybir.AluOpType.max
-ADD = mybir.AluOpType.add
-SUBTRACT = mybir.AluOpType.subtract
+MULT = mybir.AluOpType.mult
 
 P = 128
 PACK = 4
@@ -27,7 +27,7 @@ CHUNK = 256
 CHUNKS = S // CHUNK
 X_VECTOR_COLS = (0, 640, 0, 640, 0, 640, 0, 640)
 W_SCALAR_COLS = 64
-GP = (4, 4, 0, 0)
+PE_JOINED = 2
 
 
 def tile_picked_bev_max_e_kernel(
@@ -50,6 +50,10 @@ def tile_picked_bev_max_e_kernel(
         for t in range(PACK):
             nc.vector.memset(maps[0][t][:].bitcast(I32), 0)
             nc.gpsimd.memset(maps[1][t][:].bitcast(I32), 0)
+        identity = held.tile([P, P], F32, name="identity")
+        make_identity(nc, identity[:])
+        minus_one = held.tile([P, V], F32, name="minus_one")
+        nc.gpsimd.memset(minus_one[:], -1.0)
         w3_codes = held.tile([P, N], U32, name="w3_codes", align_bytes=64)
         w3_scale = held.tile([P, N], U8, name="w3_scale", align_bytes=64)
         nc.vector.memset(w3_scale[:].bitcast(I32), 0)
@@ -162,7 +166,10 @@ def tile_picked_bev_max_e_kernel(
             nc.scalar.activation(dst, banks[s][t][:], RELU)
 
         def scatter(s, t, src):
-            nc.vector.tensor_copy(maps[s][t][:].indirect(cell_lists[s][:]), src)
+            if s == 1 and t < PE_JOINED:
+                nc.vector.tensor_tensor(maps[s][t][:].indirect(cell_lists[s][:]), src, minus_one[:], MULT)
+            else:
+                nc.vector.tensor_copy(maps[s][t][:].indirect(cell_lists[s][:]), src)
 
         for g in range(PASSES):
             for t in range(PACK):
@@ -193,28 +200,61 @@ def tile_picked_bev_max_e_kernel(
 
         z_planes = [held.tile([P, PACK, CHUNK], BF16, name="zp%d" % c) for c in range(CHUNKS)]
 
-        def join(t):
-            n_gp = GP[t]
-            if n_gp:
-                cells = slice(0, n_gp * CHUNK)
-                diff = held.tile([P, 2, S], F32, name="diff%d" % t, tag="pairs%d_%d" % (t // 2, t % 2))
-                for c0 in range(0, n_gp, 2):
-                    cells = slice(c0 * CHUNK, (c0 + 2) * CHUNK)
-                    nc.gpsimd.tensor_tensor(diff[:, 0, cells], maps[0][t][:, cells], maps[1][t][:, cells], SUBTRACT)
-                    nc.scalar.activation(diff[:, 1, cells], diff[:, 0, cells], RELU)
-                for c in range(n_gp):
-                    cells = slice(c * CHUNK, (c + 1) * CHUNK)
-                    nc.gpsimd.tensor_tensor(z_planes[c][:, t, :], diff[:, 1, cells], maps[1][t][:, cells], ADD)
-            for c in range(n_gp, CHUNKS):
+        more = held.tile([P, 2, V], F32, name="more_values", tag="pairs0_0")
+        second = [values[0][:], values[1][:], more[:, 0, :], more[:, 1, :]]
+        for t in range(PACK):
+            relu(1, t, second[t])
+
+        HALF = S // 2
+        BLOCKS = HALF // P
+        a_turned = [w2_pieces[PASSES - 1][:, 1:3, :]]
+        for t in range(1, PE_JOINED):
+            a_turned.append(held.tile([P, 2, HALF], F32, name="a_turned%d" % t, tag="pairs%d_%d" % (t // 2, t % 2))[:])
+        excess = held.tile([P, 2, HALF], F32, name="excess", tag="pairs1_1")
+
+        def turn(bank, sources):
+            for b in range(BLOCKS):
+                cols = slice(b * P, (b + 1) * P)
+                for i, src in enumerate(sources):
+                    nc.tensor.matmul(
+                        bank[:, cols], lhsT=src[:, cols], rhs=identity[:], is_transpose=True, start=(i == 0), stop=(i == len(sources) - 1)
+                    )
+
+        def turn_a(t):
+            for h in range(2):
+                bank = psum.tile([P, HALF], F32, name="at%d_%d" % (t, h), tag="bank%d" % h)
+                turn(bank, [maps[0][t][:, h * HALF : (h + 1) * HALF]])
+                nc.scalar.copy(a_turned[t][:, h, :], bank[:])
+
+        def join_on_tensor(t):
+            for h in range(2):
+                cells = slice(h * HALF, (h + 1) * HALF)
+                bank = psum.tile([P, HALF], F32, name="d%d_%d" % (t, h), tag="bank%d" % (4 + h))
+                turn(bank, [maps[0][t][:, cells], maps[1][t][:, cells]])
+                nc.scalar.activation(excess[:, h, :], bank[:], RELU, scale=-1.0)
+            for h in range(2):
+                bank = psum.tile([P, HALF], F32, name="z%d_%d" % (t, h), tag="bank%d" % (6 + h))
+                turn(bank, [excess[:, h, :], a_turned[t][:, h, :]])
+                for c in range(2):
+                    nc.scalar.copy(z_planes[2 * h + c][:, t, :], bank[:, c * CHUNK : (c + 1) * CHUNK])
+
+        def join_on_vector(t):
+            for c in range(CHUNKS):
                 cells = slice(c * CHUNK, (c + 1) * CHUNK)
                 nc.vector.tensor_tensor(z_planes[c][:, t, :], maps[0][t][:, cells], maps[1][t][:, cells], MAX)
 
-        rest = [(1, 0), (1, 1), (0, 3), (1, 2), (1, 3)]
-        for i, (s, t) in enumerate(rest):
-            relu(s, t, values[i % 2][:])
-            scatter(s, t, values[i % 2][:])
-            if (1 - s, t) not in rest[i:]:
-                join(t)
+        for t in range(PE_JOINED):
+            turn_a(t)
+        for t in range(PACK - 1):
+            scatter(1, t, second[t])
+            if t < PE_JOINED:
+                join_on_tensor(t)
+            else:
+                join_on_vector(t)
+        scatter(1, 3, second[3])
+        relu(0, 3, a_turned[0][:, 0, :])
+        scatter(0, 3, a_turned[0][:, 0, :])
+        join_on_vector(3)
 
         out_rows = out.rearrange("(m p) r -> p m r", p=P)
         z_woven = [held.tile([P, PACK * CHUNK], BF16, name="zw%d" % c, align_bytes=64) for c in range(CHUNKS)]
@@ -252,7 +292,7 @@ def tile_picked_bev_max_e_kernel(
                 nc.vector.tensor_copy(staged[:, 0, :], accs[0])
                 nc.scalar.copy(staged[:, 1, :], accs[1])
             else:
-                copy_on(("scalar", "scalar", "scalar")[c], staged[:], acc[:])
+                copy_on(("scalar", "scalar", "vector")[c], staged[:], acc[:])
             nc.sync.dma_start(out=out_rows[:, :, c * CHUNK : (c + 1) * CHUNK], in_=staged[:])
 
         weave_z("scalar", 0, 0, CHUNK)

@@ -13,6 +13,7 @@ U32 = mybir.dt.uint32
 U16 = mybir.dt.uint16
 U8 = mybir.dt.uint8
 FP8X4 = mybir.dt.float8_e4m3fn_x4
+COPY = mybir.ActivationFunctionType.Copy
 RELU = mybir.ActivationFunctionType.Relu
 MAX = mybir.AluOpType.max
 MULT = mybir.AluOpType.mult
@@ -21,35 +22,35 @@ P = 128
 PACK = 4
 K_PASS = P * PACK
 PASSES = K // K_PASS
-SENSORS = 2
+NEAR, FAR = 0, 1
+LIST_ROWS = 16
 X_COLS = T // 2
+W_COLS = H // 2
+HALF = S // 2
 CHUNK = 256
 CHUNKS = S // CHUNK
-X_VECTOR_COLS = (0, 640, 0, 640, 0, 640, 0, 640)
-W_SCALAR_COLS = 64
-PE_JOINED = 2
+M_TILES = N // P
+X_VECTOR_COLS = 704
+X_VECTOR_COLS_BUSY = 256
+TENSOR_PLANES = 2
 
 
 def tile_picked_bev_max_e_kernel(
     tc, xT, w1, w2, w3_words, w3_scales, offs, near, far, out
 ):
     nc = tc.nc
+    sensors, planes, last_pass = (NEAR, FAR), range(PACK), PASSES - 1
     with ExitStack() as ctx:
         held = ctx.enter_context(tc.tile_pool(name="held", bufs=1))
         psum = ctx.enter_context(tc.psum_pool(name="psum", bufs=1))
 
-        offs_sb = held.tile([P, S // 16], U16, name="offs_sb")
-        cell_lists = [held.tile([P, V // 16], U16, name="cells%d" % s) for s in range(SENSORS)]
+        offs_sb = held.tile([P, S // LIST_ROWS], U16, name="offs_sb")
+        cell_lists = [held.tile([P, V // LIST_ROWS], U16, name="cells%d" % s) for s in sensors]
 
-        warm_in = held.tile([P, 2], F32, name="warm_in")
-        warm_out = held.tile([P, 2], F32, name="warm_out")
-        nc.vector.memset(warm_in[:], 0.0)
-        nc.scalar.activation(warm_out[:], warm_in[:], RELU)
-
-        maps = [[held.tile([P, S], F32, name="map%d_%d" % (s, t)) for t in range(PACK)] for s in range(SENSORS)]
-        for t in range(PACK):
-            nc.vector.memset(maps[0][t][:].bitcast(I32), 0)
-            nc.gpsimd.memset(maps[1][t][:].bitcast(I32), 0)
+        maps = [[held.tile([P, S], F32, name="map%d_%d" % (s, t)) for t in planes] for s in sensors]
+        for t in planes:
+            nc.vector.memset(maps[NEAR][t][:].bitcast(I32), 0)
+            nc.gpsimd.memset(maps[FAR][t][:].bitcast(I32), 0)
         identity = held.tile([P, P], F32, name="identity")
         make_identity(nc, identity[:])
         minus_one = held.tile([P, V], F32, name="minus_one")
@@ -58,226 +59,222 @@ def tile_picked_bev_max_e_kernel(
         w3_scale = held.tile([P, N], U8, name="w3_scale", align_bytes=64)
         nc.vector.memset(w3_scale[:].bitcast(I32), 0)
 
-        pairs = [[held.tile([P, 2 * T], BF16, name="pairs%d_%d" % (g, u), tag="pairs%d_%d" % (g, u)) for u in range(2)] for g in range(PASSES)]
-        x_codes = [held.tile([P, S], U32, name="xc%d" % g, align_bytes=64) for g in range(PASSES)]
-        x_scale = [held.tile([P, S], U8, name="xs%d" % g, align_bytes=64) for g in range(PASSES)]
-        picked = [held.tile([P, 2 * S], U32, name="pk%d" % g) for g in range(PASSES)]
-        w_codes = [[held.tile([P, H], U32, name="wc%d_%d" % (s, g), align_bytes=64) for g in range(PASSES)] for s in range(SENSORS)]
-        w_scale = [[held.tile([P, H], U8, name="ws%d_%d" % (s, g), align_bytes=64) for g in range(PASSES)] for s in range(SENSORS)]
-        dealt = [[held.tile([P, PACK * H], BF16, name="dealt%d_%d" % (s, g), align_bytes=64) for g in range(PASSES)] for s in range(SENSORS)]
-        woven = held.tile([P, PACK * S], BF16, name="woven", align_bytes=64)
+        pairs = [
+            [held.tile([P, 2 * T], BF16, name="pairs%d_%d" % (g, u), tag="pairs%d_%d" % (g, u)) for u in range(2)]
+            for g in range(PASSES)
+        ]
+        x_codes = [held.tile([P, S], U32, name="x_codes%d" % g, align_bytes=64) for g in range(PASSES)]
+        x_scale = [held.tile([P, S], U8, name="x_scale%d" % g, align_bytes=64) for g in range(PASSES)]
+        picked = [held.tile([P, 2 * S], U32, name="picked%d" % g) for g in range(PASSES)]
+        w_codes = [
+            [held.tile([P, H], U32, name="w_codes%d_%d" % (s, g), align_bytes=64) for g in range(PASSES)] for s in sensors
+        ]
+        w_scale = [
+            [held.tile([P, H], U8, name="w_scale%d_%d" % (s, g), align_bytes=64) for g in range(PASSES)] for s in sensors
+        ]
+        dealt = [
+            [held.tile([P, PACK * H], BF16, name="dealt%d_%d" % (s, g), align_bytes=64) for g in range(PASSES)]
+            for s in sensors
+        ]
+        x_woven = held.tile([P, PACK * S], BF16, name="x_woven", align_bytes=64)
 
-        def copy_on(engine, dst, src):
-            if engine == "vector":
-                nc.vector.tensor_copy(dst, src)
-            else:
-                nc.scalar.copy(dst, src)
-
-        def load_x(g, u, h):
-            piece = held.tile([P, 2, X_COLS], F32, name="piece", tag="x%d" % (4 * g + 2 * u + h))
-            rows = xT[g * K_PASS : (g + 1) * K_PASS, :].rearrange("(p j) c -> p j c", j=PACK)
-            nc.sync.dma_start(out=piece[:], in_=rows[:, 2 * u : 2 * u + 2, h * X_COLS : (h + 1) * X_COLS])
-            return piece
+        def pass_rows(matrix, g):
+            return matrix[g * K_PASS : (g + 1) * K_PASS, :].rearrange("(p j) c -> p j c", j=PACK)
 
         def round_x(piece, g, u, h, vector_cols):
-            dst = pairs[g][u][:].rearrange("p (c e) -> p c e", e=2)
-            for engine, c0, c1 in (("scalar", vector_cols, X_COLS), ("vector", 0, vector_cols)):
-                if c1 > c0:
-                    copy_on(engine, dst[:, h * X_COLS + c0 : h * X_COLS + c1, :], piece[:, :, c0:c1].rearrange("p e c -> p c e"))
+            dst = pairs[g][u][:].rearrange("p (c e) -> p c e", e=2)[:, h * X_COLS : (h + 1) * X_COLS, :]
+            src = piece[:].rearrange("p e c -> p c e")
+            nc.scalar.activation(dst[:, vector_cols:, :], src[:, vector_cols:, :], COPY)
+            if vector_cols:
+                nc.vector.tensor_copy(dst[:, :vector_cols, :], src[:, :vector_cols, :])
 
         def gather_x(g, u, n0, n1):
-            nc.vector.tensor_copy(
-                picked[g][:, u * S + n0 : u * S + n1], pairs[g][u][:].bitcast(U32).indirect(offs_sb[:, n0 // 16 : n1 // 16])
-            )
+            window = pairs[g][u][:].bitcast(U32)
+            entries = offs_sb[:, n0 // LIST_ROWS : n1 // LIST_ROWS]
+            nc.vector.tensor_copy(picked[g][:, u * S + n0 : u * S + n1], window.indirect(entries))
 
-        def weave_x(g, n0, n1, dst):
+        def quantize_x(g, n0, n1, woven):
             nc.vector.tensor_copy(
-                dst.bitcast(I32).rearrange("p (n u) -> p n u", u=2),
+                woven.bitcast(I32).rearrange("p (n u) -> p n u", u=2),
                 picked[g][:].bitcast(I32).rearrange("p (u n) -> p n u", u=2)[:, n0:n1, :],
             )
+            nc.vector.quantize_mx(out=x_codes[g][:, n0:n1].bitcast(FP8X4), scales=x_scale[g][:, n0:n1], in_=woven)
 
-        def quantize_x(g, n0, n1, src):
-            nc.vector.quantize_mx(out=x_codes[g][:, n0:n1].bitcast(FP8X4), scales=x_scale[g][:, n0:n1], in_=src)
-
-        def load_w(w, g, c0, c1, piece=None):
-            if piece is None:
-                piece = held.tile([P, PACK, c1 - c0], F32, name="w1raw%d_%d" % (g, c0))
-            rows = w[g * K_PASS : (g + 1) * K_PASS, :].rearrange("(p j) c -> p j c", j=PACK)
-            nc.sync.dma_start(out=piece[:], in_=rows[:, :, c0:c1])
-            return piece
-
-        def round_w(engine, dst_tile, piece, piece_c0, c0, c1):
-            dst = dst_tile[:].rearrange("p (t m j) -> p m j t", t=PACK, j=PACK)
-            src = piece[:, :, c0 - piece_c0 : c1 - piece_c0].rearrange("p j (m t) -> p m j t", t=PACK)
-            copy_on(engine, dst[:, c0 // PACK : c1 // PACK, :, :], src)
+        def deal_views(s, g, piece, c0):
+            width = piece.shape[2]
+            dst = dealt[s][g][:].rearrange("p (t m j) -> p m j t", t=PACK, j=PACK)
+            return dst[:, c0 // PACK : (c0 + width) // PACK, :, :], piece[:].rearrange("p j (m t) -> p m j t", t=PACK)
 
         def quantize_w(s, g):
             nc.vector.quantize_mx(out=w_codes[s][g][:].bitcast(FP8X4), scales=w_scale[s][g][:], in_=dealt[s][g][:])
 
-        def first_layer_pass(acc, s, t, g):
+        for g in range(PASSES):
+            for u in range(2):
+                for h in range(2):
+                    piece = held.tile([P, 2, X_COLS], F32, name="x_piece", tag="x%d" % (4 * g + 2 * u + h))
+                    nc.sync.dma_start(
+                        out=piece[:], in_=pass_rows(xT, g)[:, 2 * u : 2 * u + 2, h * X_COLS : (h + 1) * X_COLS]
+                    )
+                    if (g, u, h) == (0, 0, 0):
+                        nc.sync.dma_start(offs_sb[:], offs)
+                    share = X_VECTOR_COLS_BUSY if (g, u) == (last_pass, 0) else X_VECTOR_COLS
+                    round_x(piece, g, u, h, share if h == 1 else 0)
+                if (g, u) != (last_pass, 1):
+                    gather_x(g, u, 0, S)
+            if g != last_pass:
+                quantize_x(g, 0, S, x_woven[:])
+        gather_x(last_pass, 1, 0, V)
+        quantize_x(last_pass, 0, V, x_woven[:, : PACK * V])
+        gather_x(last_pass, 1, V, S)
+
+        for g in range(PASSES):
+            for c0 in (0, W_COLS):
+                piece = held.tile([P, PACK, W_COLS], F32, name="w1_piece%d_%d" % (g, c0))
+                nc.sync.dma_start(out=piece[:], in_=pass_rows(w1, g)[:, :, c0 : c0 + W_COLS])
+                if (g, c0) == (last_pass, W_COLS):
+                    nc.vector.tensor_copy(*deal_views(NEAR, g, piece, c0))
+                else:
+                    nc.scalar.copy(*deal_views(NEAR, g, piece, c0))
+            quantize_w(NEAR, g)
+        quantize_x(last_pass, V, S, dealt[NEAR][last_pass][:])
+
+        banks = [
+            [psum.tile([P, V], F32, name="near%d" % t, tag="bank%d" % (t % 2)) for t in planes],
+            [psum.tile([P, V], F32, name="far%d" % t, tag="bank%d" % (PACK + t)) for t in planes],
+        ]
+        values = [held.tile([P, V], F32, name="values%d" % b) for b in range(2)]
+
+        def first_layer_pass(s, t, g):
             cols = slice(t * P, (t + 1) * P)
-            picks = slice(s * V, (s + 1) * V)
+            entries = slice(s * V, (s + 1) * V)
             nc.tensor.matmul_mx(
-                out=acc[:],
+                out=banks[s][t][:],
                 lhsT=w_codes[s][g][:, cols].bitcast(FP8X4),
                 lhsT_scale=w_scale[s][g][:, cols],
-                rhs=x_codes[g][:, picks].bitcast(FP8X4),
-                rhs_scale=x_scale[g][:, picks],
+                rhs=x_codes[g][:, entries].bitcast(FP8X4),
+                rhs_scale=x_scale[g][:, entries],
                 start=(g == 0),
-                stop=(g == PASSES - 1),
+                stop=(g == last_pass),
             )
-
-        x_steps = [(g, u, h) for g in range(PASSES) for u in range(2) for h in range(2)]
-        for i, (g, u, h) in enumerate(x_steps):
-            piece = load_x(g, u, h)
-            if i == 0:
-                nc.sync.dma_start(offs_sb[:], offs)
-            round_x(piece, g, u, h, X_VECTOR_COLS[i])
-            if h == 1 and i < len(x_steps) - 1:
-                gather_x(g, u, 0, S)
-                if u == 1:
-                    weave_x(g, 0, S, woven[:])
-                    quantize_x(g, 0, S, woven[:])
-        g_last = PASSES - 1
-        gather_x(g_last, 1, 0, V)
-        weave_x(g_last, 0, V, woven[:, : PACK * V])
-        quantize_x(g_last, 0, V, woven[:, : PACK * V])
-        gather_x(g_last, 1, V, S)
-
-        half = H // 2
-        for g in range(PASSES):
-            for c0 in (0, half):
-                piece = load_w(w1, g, c0, c0 + half)
-                if g == 0 and c0 == half:
-                    nc.sync.dma_start(cell_lists[0][:], near)
-                if g == PASSES - 1 and c0 == half:
-                    round_w("scalar", dealt[0][g], piece, c0, c0, c0 + W_SCALAR_COLS)
-                    round_w("vector", dealt[0][g], piece, c0, c0 + W_SCALAR_COLS, H)
-                else:
-                    round_w("scalar", dealt[0][g], piece, c0, c0, c0 + half)
-            quantize_w(0, g)
-        weave_x(g_last, V, S, dealt[0][g_last][:])
-        quantize_x(g_last, V, S, dealt[0][g_last][:])
-
-        banks = [[psum.tile([P, V], F32, name="acc%d_%d" % (s, t), tag="bank%d" % (s * PACK + t)) for t in range(PACK)] for s in range(SENSORS)]
-        values = [held.tile([P, V], F32, name="values%d" % b) for b in range(2)]
 
         def relu(s, t, dst):
             nc.scalar.activation(dst, banks[s][t][:], RELU)
 
         def scatter(s, t, src):
-            if s == 1 and t < PE_JOINED:
-                nc.vector.tensor_tensor(maps[s][t][:].indirect(cell_lists[s][:]), src, minus_one[:], MULT)
+            window = maps[s][t][:].indirect(cell_lists[s][:])
+            if s == FAR and t < TENSOR_PLANES:
+                nc.vector.tensor_tensor(window, src, minus_one[:], MULT)
             else:
-                nc.vector.tensor_copy(maps[s][t][:].indirect(cell_lists[s][:]), src)
+                nc.vector.tensor_copy(window, src)
 
+        for t in planes:
+            for g in range(PASSES):
+                first_layer_pass(NEAR, t, g)
+            if t < len(values):
+                relu(NEAR, t, values[t][:])
+
+        nc.sync.dma_start(cell_lists[NEAR][:], near)
+        w2_pieces = [held.tile([P, PACK, H], F32, name="w2_piece%d" % g, tag="x%d" % g) for g in range(PASSES)]
         for g in range(PASSES):
-            for t in range(PACK):
-                first_layer_pass(banks[0][t], 0, t, g)
-        for t in range(2):
-            relu(0, t, values[t][:])
-
-        w2_pieces = [load_w(w2, g, 0, H, held.tile([P, PACK, H], F32, name="w2raw%d" % g, tag="x%d" % g)) for g in range(PASSES)]
-        nc.sync.dma_start(cell_lists[1][:], far)
+            nc.sync.dma_start(out=w2_pieces[g][:], in_=pass_rows(w2, g))
+        nc.sync.dma_start(cell_lists[FAR][:], far)
         nc.sync.dma_start(out=w3_codes[:].bitcast(I32), in_=w3_words[0].rearrange("p n r -> p (n r)").bitcast(I32))
         for q in range(4):
             nc.sync.dma_start(
                 out=w3_scale[32 * q : 32 * q + 4, :].bitcast(I32), in_=w3_scales[0, 4 * q : 4 * q + 4, :].bitcast(I32)
             )
         for g in range(PASSES):
-            round_w("scalar", dealt[1][g], w2_pieces[g], 0, 0, H)
+            nc.scalar.copy(*deal_views(FAR, g, w2_pieces[g], 0))
 
-        scatter(0, 0, values[0][:])
-        scatter(0, 1, values[1][:])
+        spent_w2 = w2_pieces[last_pass]
+        scatter(NEAR, 0, values[0][:])
+        scatter(NEAR, 1, values[1][:])
         for g in range(PASSES):
-            quantize_w(1, g)
-        late = w2_pieces[PASSES - 1][:, 0, :]
-        relu(0, 2, late)
-        scatter(0, 2, late)
+            quantize_w(FAR, g)
+        relu(NEAR, 2, spent_w2[:, 0, :])
+        scatter(NEAR, 2, spent_w2[:, 0, :])
         for g in range(PASSES):
-            for t in range(PACK):
-                first_layer_pass(banks[1][t], 1, t, g)
+            for t in planes:
+                first_layer_pass(FAR, t, g)
 
-        z_planes = [held.tile([P, PACK, CHUNK], BF16, name="zp%d" % c) for c in range(CHUNKS)]
+        z_planes = [held.tile([P, PACK, CHUNK], BF16, name="z_planes%d" % c, tag="z_planes%d" % c) for c in range(CHUNKS)]
 
-        more = held.tile([P, 2, V], F32, name="more_values", tag="pairs0_0")
-        second = [values[0][:], values[1][:], more[:, 0, :], more[:, 1, :]]
-        for t in range(PACK):
-            relu(1, t, second[t])
+        more_values = held.tile([P, 2, V], F32, name="more_values", tag="pairs0_0")
+        far_values = [values[0][:], values[1][:], more_values[:, 0, :], more_values[:, 1, :]]
+        for t in planes:
+            relu(FAR, t, far_values[t])
 
-        HALF = S // 2
-        BLOCKS = HALF // P
-        a_turned = [w2_pieces[PASSES - 1][:, 1:3, :]]
-        for t in range(1, PE_JOINED):
-            a_turned.append(held.tile([P, 2, HALF], F32, name="a_turned%d" % t, tag="pairs%d_%d" % (t // 2, t % 2))[:])
+        a_turned = [spent_w2[:, 1:3, :], held.tile([P, 2, HALF], F32, name="a_turned1", tag="pairs0_1")[:]]
         excess = held.tile([P, 2, HALF], F32, name="excess", tag="pairs1_1")
 
-        def turn(bank, sources):
-            for b in range(BLOCKS):
+        def add_turned(bank, terms):
+            for b in range(HALF // P):
                 cols = slice(b * P, (b + 1) * P)
-                for i, src in enumerate(sources):
+                for i, term in enumerate(terms):
                     nc.tensor.matmul(
-                        bank[:, cols], lhsT=src[:, cols], rhs=identity[:], is_transpose=True, start=(i == 0), stop=(i == len(sources) - 1)
+                        bank[:, cols],
+                        lhsT=term[:, cols],
+                        rhs=identity[:],
+                        is_transpose=True,
+                        start=(i == 0),
+                        stop=(i == len(terms) - 1),
                     )
 
         def turn_a(t):
             for h in range(2):
-                bank = psum.tile([P, HALF], F32, name="at%d_%d" % (t, h), tag="bank%d" % h)
-                turn(bank, [maps[0][t][:, h * HALF : (h + 1) * HALF]])
+                bank = psum.tile([P, HALF], F32, name="a_bank", tag="bank%d" % (2 + h))
+                add_turned(bank, [maps[NEAR][t][:, h * HALF : (h + 1) * HALF]])
                 nc.scalar.copy(a_turned[t][:, h, :], bank[:])
 
-        def join_on_tensor(t):
+        def max_on_tensor(t):
             for h in range(2):
                 cells = slice(h * HALF, (h + 1) * HALF)
-                bank = psum.tile([P, HALF], F32, name="d%d_%d" % (t, h), tag="bank%d" % (4 + h))
-                turn(bank, [maps[0][t][:, cells], maps[1][t][:, cells]])
+                bank = psum.tile([P, HALF], F32, name="difference_bank", tag="bank%d" % (4 + h))
+                add_turned(bank, [maps[NEAR][t][:, cells], maps[FAR][t][:, cells]])
                 nc.scalar.activation(excess[:, h, :], bank[:], RELU, scale=-1.0)
             for h in range(2):
-                bank = psum.tile([P, HALF], F32, name="z%d_%d" % (t, h), tag="bank%d" % (6 + h))
-                turn(bank, [excess[:, h, :], a_turned[t][:, h, :]])
-                for c in range(2):
-                    nc.scalar.copy(z_planes[2 * h + c][:, t, :], bank[:, c * CHUNK : (c + 1) * CHUNK])
+                bank = psum.tile([P, HALF], F32, name="z_bank", tag="bank%d" % (6 + h))
+                add_turned(bank, [excess[:, h, :], a_turned[t][:, h, :]])
+                for c in range(HALF // CHUNK):
+                    nc.scalar.copy(z_planes[h * HALF // CHUNK + c][:, t, :], bank[:, c * CHUNK : (c + 1) * CHUNK])
 
-        def join_on_vector(t):
+        def max_on_vector(t):
             for c in range(CHUNKS):
                 cells = slice(c * CHUNK, (c + 1) * CHUNK)
-                nc.vector.tensor_tensor(z_planes[c][:, t, :], maps[0][t][:, cells], maps[1][t][:, cells], MAX)
+                nc.vector.tensor_tensor(z_planes[c][:, t, :], maps[NEAR][t][:, cells], maps[FAR][t][:, cells], MAX)
 
-        for t in range(PE_JOINED):
+        for t in range(TENSOR_PLANES):
             turn_a(t)
-        for t in range(PACK - 1):
-            scatter(1, t, second[t])
-            if t < PE_JOINED:
-                join_on_tensor(t)
+        last_plane = PACK - 1
+        for t in range(last_plane):
+            scatter(FAR, t, far_values[t])
+            if t < TENSOR_PLANES:
+                max_on_tensor(t)
             else:
-                join_on_vector(t)
-        scatter(1, 3, second[3])
-        relu(0, 3, a_turned[0][:, 0, :])
-        scatter(0, 3, a_turned[0][:, 0, :])
-        join_on_vector(3)
+                max_on_vector(t)
+        scatter(FAR, last_plane, far_values[last_plane])
+        relu(NEAR, last_plane, a_turned[0][:, 0, :])
+        scatter(NEAR, last_plane, a_turned[0][:, 0, :])
+        max_on_vector(last_plane)
 
         out_rows = out.rearrange("(m p) r -> p m r", p=P)
-        z_woven = [held.tile([P, PACK * CHUNK], BF16, name="zw%d" % c, align_bytes=64) for c in range(CHUNKS)]
+        z_woven = [held.tile([P, PACK * CHUNK], BF16, name="z_woven%d" % c, align_bytes=64) for c in range(CHUNKS)]
 
-        def weave_z(engine, c, n0, n1):
-            copy_on(
-                engine,
-                z_woven[c][:, PACK * n0 : PACK * n1].rearrange("p (c i t) -> p c t i", i=4, t=PACK),
-                z_planes[c][:, :, n0:n1].rearrange("p t (c i) -> p c t i", i=4),
+        def weave_views(c):
+            return (
+                z_woven[c][:].rearrange("p (n i t) -> p n t i", i=4, t=PACK),
+                z_planes[c][:].rearrange("p t (n i) -> p n t i", i=4),
             )
 
-        def second_layer(c):
-            last = c == CHUNKS - 1
-            z_codes = held.tile([P, CHUNK], U32, name="zc%d" % c, align_bytes=64)
-            z_scale = held.tile([P, CHUNK], U8, name="zs%d" % c, align_bytes=64)
+        staged_first = held.tile([P, 2, M_TILES, CHUNK], F32, name="staged_first", tag="z_planes2")
+        staged_last = held.tile([P, 2, M_TILES, CHUNK], F32, name="staged_last", tag="x2")
+        staged = [staged_first[:, 0], staged_first[:, 1], staged_last[:, 0], staged_last[:, 1]]
+
+        def last_layer(c, accs):
+            z_codes = held.tile([P, CHUNK], U32, name="z_codes%d" % c, align_bytes=64)
+            z_scale = held.tile([P, CHUNK], U8, name="z_scale%d" % c, align_bytes=64)
             nc.vector.quantize_mx(out=z_codes[:].bitcast(FP8X4), scales=z_scale[:], in_=z_woven[c][:])
-            staged = held.tile([P, N // P, CHUNK], F32, name="staged%d" % c, tag="x%d" % (2 + c))
-            if last:
-                accs = [psum.tile([P, CHUNK], F32, name="oacc%d_%d" % (c, m), tag="bank%d" % (c + m))[:] for m in range(N // P)]
-            else:
-                acc = psum.tile([P, N // P, CHUNK], F32, name="oacc%d" % c, tag="bank%d" % c)
-                accs = [acc[:, m, :] for m in range(N // P)]
-            for m in range(N // P):
+            for m in range(M_TILES):
                 cols = slice(m * P, (m + 1) * P)
                 nc.tensor.matmul_mx(
                     out=accs[m],
@@ -288,19 +285,26 @@ def tile_picked_bev_max_e_kernel(
                     start=True,
                     stop=True,
                 )
-            if last:
-                nc.vector.tensor_copy(staged[:, 0, :], accs[0])
-                nc.scalar.copy(staged[:, 1, :], accs[1])
-            else:
-                copy_on(("scalar", "scalar", "vector")[c], staged[:], acc[:])
-            nc.sync.dma_start(out=out_rows[:, :, c * CHUNK : (c + 1) * CHUNK], in_=staged[:])
 
-        weave_z("scalar", 0, 0, CHUNK)
-        weave_z("vector", 1, 0, CHUNK)
-        weave_z("scalar", 2, 0, CHUNK)
-        second_layer(0)
-        second_layer(1)
-        weave_z("vector", 3, 0, 160)
-        weave_z("scalar", 3, 160, CHUNK)
-        second_layer(2)
-        second_layer(3)
+        def store(c):
+            nc.sync.dma_start(out=out_rows[:, :, c * CHUNK : (c + 1) * CHUNK], in_=staged[c])
+
+        def chunk_in_one_bank(c, copy_out):
+            acc = psum.tile([P, M_TILES, CHUNK], F32, name="out_bank%d" % c, tag="bank%d" % c)
+            last_layer(c, [acc[:, m, :] for m in range(M_TILES)])
+            copy_out(staged[c], acc[:])
+            store(c)
+
+        nc.scalar.copy(*weave_views(0))
+        nc.vector.tensor_copy(*weave_views(1))
+        nc.scalar.copy(*weave_views(2))
+        chunk_in_one_bank(0, nc.scalar.copy)
+        chunk_in_one_bank(1, nc.scalar.copy)
+        nc.vector.tensor_copy(*weave_views(3))
+        chunk_in_one_bank(2, nc.vector.tensor_copy)
+        last_chunk = CHUNKS - 1
+        accs = [psum.tile([P, CHUNK], F32, name="out_last%d" % m, tag="bank%d" % (last_chunk + m))[:] for m in range(M_TILES)]
+        last_layer(last_chunk, accs)
+        nc.vector.tensor_copy(staged[last_chunk][:, 0, :], accs[0])
+        nc.scalar.copy(staged[last_chunk][:, 1, :], accs[1])
+        store(last_chunk)

from contextlib import ExitStack

import concourse.mybir as mybir
from concourse.masks import make_identity

K, T, S, H, N, V = 1024, 2048, 1024, 512, 256, 512
FLOPS = 2 * (2 * K * H * V) + 2 * H * N * S

F32 = mybir.dt.float32
BF16 = mybir.dt.bfloat16
I32 = mybir.dt.int32
U32 = mybir.dt.uint32
U16 = mybir.dt.uint16
U8 = mybir.dt.uint8
FP8X4 = mybir.dt.float8_e4m3fn_x4
COPY = mybir.ActivationFunctionType.Copy
RELU = mybir.ActivationFunctionType.Relu
MAX = mybir.AluOpType.max
MULT = mybir.AluOpType.mult

P = 128
PACK = 4
K_PASS = P * PACK
PASSES = K // K_PASS
NEAR, FAR = 0, 1
LIST_ROWS = 16
X_COLS = T // 2
W_COLS = H // 2
HALF = S // 2
CHUNK = 256
CHUNKS = S // CHUNK
M_TILES = N // P
X_VECTOR_COLS = 704
X_VECTOR_COLS_BUSY = 256
TENSOR_PLANES = 2


def tile_picked_bev_max_e_kernel(
    tc, xT, w1, w2, w3_words, w3_scales, offs, near, far, out
):
    nc = tc.nc
    sensors, planes, last_pass = (NEAR, FAR), range(PACK), PASSES - 1
    with ExitStack() as ctx:
        held = ctx.enter_context(tc.tile_pool(name="held", bufs=1))
        psum = ctx.enter_context(tc.psum_pool(name="psum", bufs=1))

        offs_sb = held.tile([P, S // LIST_ROWS], U16, name="offs_sb")
        cell_lists = [held.tile([P, V // LIST_ROWS], U16, name="cells%d" % s) for s in sensors]

        maps = [[held.tile([P, S], F32, name="map%d_%d" % (s, t)) for t in planes] for s in sensors]
        for t in planes:
            nc.vector.memset(maps[NEAR][t][:].bitcast(I32), 0)
            nc.gpsimd.memset(maps[FAR][t][:].bitcast(I32), 0)
        identity = held.tile([P, P], F32, name="identity")
        make_identity(nc, identity[:])
        minus_one = held.tile([P, V], F32, name="minus_one")
        nc.gpsimd.memset(minus_one[:], -1.0)
        w3_codes = held.tile([P, N], U32, name="w3_codes", align_bytes=64)
        w3_scale = held.tile([P, N], U8, name="w3_scale", align_bytes=64)
        nc.vector.memset(w3_scale[:].bitcast(I32), 0)

        pairs = [
            [held.tile([P, 2 * T], BF16, name="pairs%d_%d" % (g, u), tag="pairs%d_%d" % (g, u)) for u in range(2)]
            for g in range(PASSES)
        ]
        x_codes = [held.tile([P, S], U32, name="x_codes%d" % g, align_bytes=64) for g in range(PASSES)]
        x_scale = [held.tile([P, S], U8, name="x_scale%d" % g, align_bytes=64) for g in range(PASSES)]
        picked = [held.tile([P, 2 * S], U32, name="picked%d" % g) for g in range(PASSES)]
        w_codes = [
            [held.tile([P, H], U32, name="w_codes%d_%d" % (s, g), align_bytes=64) for g in range(PASSES)] for s in sensors
        ]
        w_scale = [
            [held.tile([P, H], U8, name="w_scale%d_%d" % (s, g), align_bytes=64) for g in range(PASSES)] for s in sensors
        ]
        dealt = [
            [held.tile([P, PACK * H], BF16, name="dealt%d_%d" % (s, g), align_bytes=64) for g in range(PASSES)]
            for s in sensors
        ]
        x_woven = held.tile([P, PACK * S], BF16, name="x_woven", align_bytes=64)

        def pass_rows(matrix, g):
            return matrix[g * K_PASS : (g + 1) * K_PASS, :].rearrange("(p j) c -> p j c", j=PACK)

        def round_x(piece, g, u, h, vector_cols):
            dst = pairs[g][u][:].rearrange("p (c e) -> p c e", e=2)[:, h * X_COLS : (h + 1) * X_COLS, :]
            src = piece[:].rearrange("p e c -> p c e")
            nc.scalar.activation(dst[:, vector_cols:, :], src[:, vector_cols:, :], COPY)
            if vector_cols:
                nc.vector.tensor_copy(dst[:, :vector_cols, :], src[:, :vector_cols, :])

        def gather_x(g, u, n0, n1):
            window = pairs[g][u][:].bitcast(U32)
            entries = offs_sb[:, n0 // LIST_ROWS : n1 // LIST_ROWS]
            nc.vector.tensor_copy(picked[g][:, u * S + n0 : u * S + n1], window.indirect(entries))

        def quantize_x(g, n0, n1, woven):
            nc.vector.tensor_copy(
                woven.bitcast(I32).rearrange("p (n u) -> p n u", u=2),
                picked[g][:].bitcast(I32).rearrange("p (u n) -> p n u", u=2)[:, n0:n1, :],
            )
            nc.vector.quantize_mx(out=x_codes[g][:, n0:n1].bitcast(FP8X4), scales=x_scale[g][:, n0:n1], in_=woven)

        def deal_views(s, g, piece, c0):
            width = piece.shape[2]
            dst = dealt[s][g][:].rearrange("p (t m j) -> p m j t", t=PACK, j=PACK)
            return dst[:, c0 // PACK : (c0 + width) // PACK, :, :], piece[:].rearrange("p j (m t) -> p m j t", t=PACK)

        def quantize_w(s, g):
            nc.vector.quantize_mx(out=w_codes[s][g][:].bitcast(FP8X4), scales=w_scale[s][g][:], in_=dealt[s][g][:])

        for g in range(PASSES):
            for u in range(2):
                for h in range(2):
                    piece = held.tile([P, 2, X_COLS], F32, name="x_piece", tag="x%d" % (4 * g + 2 * u + h))
                    nc.sync.dma_start(
                        out=piece[:], in_=pass_rows(xT, g)[:, 2 * u : 2 * u + 2, h * X_COLS : (h + 1) * X_COLS]
                    )
                    if (g, u, h) == (0, 0, 0):
                        nc.sync.dma_start(offs_sb[:], offs)
                    share = X_VECTOR_COLS_BUSY if (g, u) == (last_pass, 0) else X_VECTOR_COLS
                    round_x(piece, g, u, h, share if h == 1 else 0)
                if (g, u) != (last_pass, 1):
                    gather_x(g, u, 0, S)
            if g != last_pass:
                quantize_x(g, 0, S, x_woven[:])
        gather_x(last_pass, 1, 0, V)
        quantize_x(last_pass, 0, V, x_woven[:, : PACK * V])
        gather_x(last_pass, 1, V, S)

        for g in range(PASSES):
            for c0 in (0, W_COLS):
                piece = held.tile([P, PACK, W_COLS], F32, name="w1_piece%d_%d" % (g, c0))
                nc.sync.dma_start(out=piece[:], in_=pass_rows(w1, g)[:, :, c0 : c0 + W_COLS])
                if (g, c0) == (last_pass, W_COLS):
                    nc.vector.tensor_copy(*deal_views(NEAR, g, piece, c0))
                else:
                    nc.scalar.copy(*deal_views(NEAR, g, piece, c0))
            quantize_w(NEAR, g)
        quantize_x(last_pass, V, S, dealt[NEAR][last_pass][:])

        banks = [
            [psum.tile([P, V], F32, name="near%d" % t, tag="bank%d" % (t % 2)) for t in planes],
            [psum.tile([P, V], F32, name="far%d" % t, tag="bank%d" % (PACK + t)) for t in planes],
        ]
        values = [held.tile([P, V], F32, name="values%d" % b) for b in range(2)]

        def first_layer_pass(s, t, g):
            cols = slice(t * P, (t + 1) * P)
            entries = slice(s * V, (s + 1) * V)
            nc.tensor.matmul_mx(
                out=banks[s][t][:],
                lhsT=w_codes[s][g][:, cols].bitcast(FP8X4),
                lhsT_scale=w_scale[s][g][:, cols],
                rhs=x_codes[g][:, entries].bitcast(FP8X4),
                rhs_scale=x_scale[g][:, entries],
                start=(g == 0),
                stop=(g == last_pass),
            )

        def relu(s, t, dst):
            nc.scalar.activation(dst, banks[s][t][:], RELU)

        def scatter(s, t, src):
            window = maps[s][t][:].indirect(cell_lists[s][:])
            if s == FAR and t < TENSOR_PLANES:
                nc.vector.tensor_tensor(window, src, minus_one[:], MULT)
            else:
                nc.vector.tensor_copy(window, src)

        for t in planes:
            for g in range(PASSES):
                first_layer_pass(NEAR, t, g)
            if t < len(values):
                relu(NEAR, t, values[t][:])

        nc.sync.dma_start(cell_lists[NEAR][:], near)
        w2_pieces = [held.tile([P, PACK, H], F32, name="w2_piece%d" % g, tag="x%d" % g) for g in range(PASSES)]
        for g in range(PASSES):
            nc.sync.dma_start(out=w2_pieces[g][:], in_=pass_rows(w2, g))
        nc.sync.dma_start(cell_lists[FAR][:], far)
        nc.sync.dma_start(out=w3_codes[:].bitcast(I32), in_=w3_words[0].rearrange("p n r -> p (n r)").bitcast(I32))
        for q in range(4):
            nc.sync.dma_start(
                out=w3_scale[32 * q : 32 * q + 4, :].bitcast(I32), in_=w3_scales[0, 4 * q : 4 * q + 4, :].bitcast(I32)
            )
        for g in range(PASSES):
            nc.scalar.copy(*deal_views(FAR, g, w2_pieces[g], 0))

        spent_w2 = w2_pieces[last_pass]
        scatter(NEAR, 0, values[0][:])
        scatter(NEAR, 1, values[1][:])
        for g in range(PASSES):
            quantize_w(FAR, g)
        relu(NEAR, 2, spent_w2[:, 0, :])
        scatter(NEAR, 2, spent_w2[:, 0, :])
        for g in range(PASSES):
            for t in planes:
                first_layer_pass(FAR, t, g)

        z_planes = [held.tile([P, PACK, CHUNK], BF16, name="z_planes%d" % c, tag="z_planes%d" % c) for c in range(CHUNKS)]

        more_values = held.tile([P, 2, V], F32, name="more_values", tag="pairs0_0")
        far_values = [values[0][:], values[1][:], more_values[:, 0, :], more_values[:, 1, :]]
        for t in planes:
            relu(FAR, t, far_values[t])

        a_turned = [spent_w2[:, 1:3, :], held.tile([P, 2, HALF], F32, name="a_turned1", tag="pairs0_1")[:]]
        excess = held.tile([P, 2, HALF], F32, name="excess", tag="pairs1_1")

        def add_turned(bank, terms):
            for b in range(HALF // P):
                cols = slice(b * P, (b + 1) * P)
                for i, term in enumerate(terms):
                    nc.tensor.matmul(
                        bank[:, cols],
                        lhsT=term[:, cols],
                        rhs=identity[:],
                        is_transpose=True,
                        start=(i == 0),
                        stop=(i == len(terms) - 1),
                    )

        def turn_a(t):
            for h in range(2):
                bank = psum.tile([P, HALF], F32, name="a_bank", tag="bank%d" % (2 + h))
                add_turned(bank, [maps[NEAR][t][:, h * HALF : (h + 1) * HALF]])
                nc.scalar.copy(a_turned[t][:, h, :], bank[:])

        def max_on_tensor(t):
            for h in range(2):
                cells = slice(h * HALF, (h + 1) * HALF)
                bank = psum.tile([P, HALF], F32, name="difference_bank", tag="bank%d" % (4 + h))
                add_turned(bank, [maps[NEAR][t][:, cells], maps[FAR][t][:, cells]])
                nc.scalar.activation(excess[:, h, :], bank[:], RELU, scale=-1.0)
            for h in range(2):
                bank = psum.tile([P, HALF], F32, name="z_bank", tag="bank%d" % (6 + h))
                add_turned(bank, [excess[:, h, :], a_turned[t][:, h, :]])
                for c in range(HALF // CHUNK):
                    nc.scalar.copy(z_planes[h * HALF // CHUNK + c][:, t, :], bank[:, c * CHUNK : (c + 1) * CHUNK])

        def max_on_vector(t):
            for c in range(CHUNKS):
                cells = slice(c * CHUNK, (c + 1) * CHUNK)
                nc.vector.tensor_tensor(z_planes[c][:, t, :], maps[NEAR][t][:, cells], maps[FAR][t][:, cells], MAX)

        for t in range(TENSOR_PLANES):
            turn_a(t)
        last_plane = PACK - 1
        for t in range(last_plane):
            scatter(FAR, t, far_values[t])
            if t < TENSOR_PLANES:
                max_on_tensor(t)
            else:
                max_on_vector(t)
        scatter(FAR, last_plane, far_values[last_plane])
        relu(NEAR, last_plane, a_turned[0][:, 0, :])
        scatter(NEAR, last_plane, a_turned[0][:, 0, :])
        max_on_vector(last_plane)

        out_rows = out.rearrange("(m p) r -> p m r", p=P)
        z_woven = [held.tile([P, PACK * CHUNK], BF16, name="z_woven%d" % c, align_bytes=64) for c in range(CHUNKS)]

        def weave_views(c):
            return (
                z_woven[c][:].rearrange("p (n i t) -> p n t i", i=4, t=PACK),
                z_planes[c][:].rearrange("p t (n i) -> p n t i", i=4),
            )

        staged_first = held.tile([P, 2, M_TILES, CHUNK], F32, name="staged_first", tag="z_planes2")
        staged_last = held.tile([P, 2, M_TILES, CHUNK], F32, name="staged_last", tag="x2")
        staged = [staged_first[:, 0], staged_first[:, 1], staged_last[:, 0], staged_last[:, 1]]

        def last_layer(c, accs):
            z_codes = held.tile([P, CHUNK], U32, name="z_codes%d" % c, align_bytes=64)
            z_scale = held.tile([P, CHUNK], U8, name="z_scale%d" % c, align_bytes=64)
            nc.vector.quantize_mx(out=z_codes[:].bitcast(FP8X4), scales=z_scale[:], in_=z_woven[c][:])
            for m in range(M_TILES):
                cols = slice(m * P, (m + 1) * P)
                nc.tensor.matmul_mx(
                    out=accs[m],
                    lhsT=w3_codes[:, cols].bitcast(FP8X4),
                    lhsT_scale=w3_scale[:, cols],
                    rhs=z_codes[:].bitcast(FP8X4),
                    rhs_scale=z_scale[:],
                    start=True,
                    stop=True,
                )

        def store(c):
            nc.sync.dma_start(out=out_rows[:, :, c * CHUNK : (c + 1) * CHUNK], in_=staged[c])

        def chunk_in_one_bank(c, copy_out):
            acc = psum.tile([P, M_TILES, CHUNK], F32, name="out_bank%d" % c, tag="bank%d" % c)
            last_layer(c, [acc[:, m, :] for m in range(M_TILES)])
            copy_out(staged[c], acc[:])
            store(c)

        nc.scalar.copy(*weave_views(0))
        nc.vector.tensor_copy(*weave_views(1))
        nc.scalar.copy(*weave_views(2))
        chunk_in_one_bank(0, nc.scalar.copy)
        chunk_in_one_bank(1, nc.scalar.copy)
        nc.vector.tensor_copy(*weave_views(3))
        chunk_in_one_bank(2, nc.vector.tensor_copy)
        last_chunk = CHUNKS - 1
        accs = [psum.tile([P, CHUNK], F32, name="out_last%d" % m, tag="bank%d" % (last_chunk + m))[:] for m in range(M_TILES)]
        last_layer(last_chunk, accs)
        nc.vector.tensor_copy(staged[last_chunk][:, 0, :], accs[0])
        nc.scalar.copy(staged[last_chunk][:, 1, :], accs[1])
        store(last_chunk)
